import numpy as np
import ml_dtypes


def mxq(x, axis, fmt="e4m3"):
    dtype, down = {"e4m3": (ml_dtypes.float8_e4m3fn, 7), "e5m2": (ml_dtypes.float8_e5m2, 14)}[fmt]
    v = np.moveaxis(np.asarray(x, np.float32).astype(ml_dtypes.bfloat16).astype(np.float64), axis, -1)
    blocks = v.reshape(v.shape[:-1] + (-1, 32))
    amax = np.abs(blocks).max(-1, keepdims=True)
    byte = np.maximum(np.where(amax > 0, np.frexp(amax)[1] - 1 + 127, 0) - down, 1)
    scale = np.exp2(byte - 127.0)
    codes = (blocks / scale).astype(np.float32).astype(dtype).astype(np.float64)
    return np.moveaxis((codes * scale).reshape(v.shape), -1, axis)


WIDE = False


def mx_kscale(k):
    if not WIDE:
        return np.ones(k)
    levels = np.array([30, -30])
    if k % 512:
        return np.exp2(np.random.permutation(np.resize(levels, k // 32))).repeat(32)
    a = np.empty((k // 512, 16))
    for p in range(k // 512):
        a[p, :8] = np.random.permutation(np.resize(levels, 8))
        for g in range(8):
            far = levels[np.abs(levels - a[p, g]) >= 10]
            a[p, g + 8] = far[np.random.randint(len(far))]
    return np.exp2(a.ravel()).repeat(32)


BF16 = ml_dtypes.bfloat16


def bf(x):
    return np.asarray(x, np.float32).astype(BF16)


def f64(x):
    return np.asarray(x).astype(np.float64)


T, E, P, D, F = 2048, 4, 128, 1024, 1024


def silu(v):
    return v / (1.0 + np.exp(-v))


def setup_inputs():
    s, t = mx_kscale(T), mx_kscale(D)
    return {"logits": bf(2.0 * np.random.standard_normal((T, E * P))),
            "token_gain": bf((1.0 + 0.2 * np.random.standard_normal(T)) * s),
            "x": bf(np.random.standard_normal((T, D)) / s[:, None]),
            "slot_embed": bf(0.2 * np.random.standard_normal((E * P, D))),
            "norm_gain": bf((1.0 + 0.1 * np.random.standard_normal((E, D))) * t),
            "w_gate": bf(np.random.standard_normal((E, D, F)) / np.sqrt(D) / t[:, None]),
            "b_gate": bf(0.3 * np.random.standard_normal((E, F))),
            "w_up": bf(np.random.standard_normal((E, D, F)) / np.sqrt(D) / t[:, None])}


def reference(logits, token_gain, x, slot_embed, norm_gain, w_gate, b_gate, w_up):
    l = f64(logits)
    a = np.exp(l - l.max(axis=0, keepdims=True))
    total = a.sum(axis=0)
    disp = a * f64(token_gain)[:, None]
    mix = mxq(disp, 0, "e4m3").T @ mxq(f64(x), 0, "e4m3")
    slots = mix / total[:, None] + f64(slot_embed)
    z = slots / np.sqrt(np.mean(np.square(slots), axis=1, keepdims=True))
    z = z.reshape(E, P, D) * f64(norm_gain)[:, None, :]
    zq = mxq(z.reshape(E * P, D), 1, "e5m2")
    wg, wu, bg = f64(w_gate), f64(w_up), f64(b_gate)
    hidden = []
    for e in range(E):
        gate = (zq.reshape(E, P, D)[e] @ mxq(wg[e], 0, "e4m3")) + bg[e]
        up = zq.reshape(E, P, D)[e] @ mxq(wu[e], 0, "e4m3")
        hidden.append(silu(gate) * up)
    return np.stack(hidden)

@@ -1,0 +1,377 @@
+from contextlib import ExitStack
+
+import concourse.mybir as mybir
+from concourse.masks import make_identity
+
+F32 = mybir.dt.float32
+BF16 = mybir.dt.bfloat16
+U32 = mybir.dt.uint32
+U8 = mybir.dt.uint8
+E4 = mybir.dt.float8_e4m3fn_x4
+E5 = mybir.dt.float8_e5m2_x4
+ACT = mybir.ActivationFunctionType
+ALU = mybir.AluOpType
+AX = mybir.AxisListType
+
+T, E, P, D, F = 2048, 4, 128, 1024, 1024
+S = E * P
+G = T // 512
+FLOPS = 2 * T * S * D + 4 * S * D * F
+
+X_OWN = 'SSVVSVSV'
+W_OWN = 'SSSSSVVSVVVSSSVSVSVSSVSSVVSVSSVS'
+X_IL = [-2,-2,0,0,4,9,12,15]
+X_Q = [5,3,3,2,16,10,12,16]
+LAG = 2
+GRP = 7
+D_SLOT = [0,1,3,4]
+
+
+def tile_soft_moe_dispatch_f3_kernel(tc, logits, token_gain, x, slot_embed, norm_gain, w_gate, b_gate, w_up, out):
+    nc = tc.nc
+    with ExitStack() as ctx:
+        one = ctx.enter_context(tc.tile_pool(name="one", bufs=1))
+        ring = ctx.enter_context(tc.tile_pool(name="ring", bufs=2))
+        psum = ctx.enter_context(tc.psum_pool(name="psum", bufs=8))
+
+        def bank(shape, dtype):
+            return psum.tile(shape, dtype, name="bank", tag="bank", bufs=8)
+
+        warm = one.tile([P, 1], F32, name="warm")
+        nc.vector.memset(warm[:], 0.0)
+        warm2 = one.tile([P, 1], F32, name="warm2")
+        nc.scalar.activation(warm2[:], warm[:], ACT.Exp)
+        gain = one.tile([P, G, 4], BF16, name="gain")
+        nc.scalar.dma_start(out=gain[:], in_=token_gain.rearrange("(g p j) -> p g j", p=P, j=4))
+        ident = one.tile([P, P], BF16, name="ident")
+        make_identity(nc, ident[:])
+        ident32 = one.tile([P, P], F32, name="ident32")
+        make_identity(nc, ident32[:])
+        mhalf = one.tile([P, 1], F32, name="mhalf")
+        nc.gpsimd.memset(mhalf[:], -0.5)
+
+        xv = x.rearrange("(g p j) d -> g p j d", p=P, j=4)
+        lv = logits.rearrange("(g p j) s -> g p j s", p=P, j=4)
+        raws = {}
+
+        def load_raw(key, src, split=False):
+            r = ring.tile([P, 4, 1024], BF16, name="raw", tag="raw", bufs=6)
+            if split:
+                nc.sync.dma_start(out=r[:, :, 0:512], in_=src[:, :, 0:512])
+            else:
+                nc.sync.dma_start(out=r[:], in_=src)
+            raws[key] = r
+
+        lg = []
+        load_raw(("x", 0), xv[0], split=True)
+        for g in range(G):
+            t = one.tile([P, 4, S], BF16, name="lg%d" % g)
+            nc.sync.dma_start(out=t[:], in_=lv[g])
+            lg.append(t)
+        nc.sync.dma_start(out=raws[("x", 0)][:, :, 512:1024], in_=xv[0][:, :, 512:1024])
+        for g in range(1, G):
+            load_raw(("x", g), xv[g])
+        emb = one.tile([P, E, D], BF16, name="emb")
+        nc.sync.dma_start(out=emb[:], in_=slot_embed.rearrange("(e p) d -> p e d", p=P))
+        ng = one.tile([P, E * D], BF16, name="ng")
+        nc.sync.dma_start(out=ng[:], in_=norm_gain.rearrange("e d -> (e d)").partition_broadcast(P))
+        bg = one.tile([P, E * F], BF16, name="bg")
+
+        wsrc = []
+        for e in range(E):
+            for m, w in enumerate((w_gate, w_up)):
+                wv = w[e].rearrange("(c p j) f -> c p j f", p=P, j=4)
+                for c in range(2):
+                    wsrc.append(wv[c])
+        loaded = []
+
+        def next_load():
+            i = len(loaded)
+            if i < len(wsrc):
+                load_raw(("w", i), wsrc[i])
+                loaded.append(i)
+
+        next_load()
+        next_load()
+        nc.sync.dma_start(out=bg[:], in_=b_gate.rearrange("e d -> (e d)").partition_broadcast(P))
+
+        groups = {}
+        pas = {}
+
+        def pass_through(key, tile_key, h):
+            for q in range(2):
+                bk = bank([P, 256, 4], BF16)
+                c0 = 512 * h + 256 * q
+                for j in range(4):
+                    nc.tensor.matmul(bk[:, :, j], lhsT=ident[:], rhs=raws[tile_key][:, j, c0 : c0 + 256], start=True, stop=True)
+                pas[(key, q)] = bk
+
+        def interleave(key, tile_key, h, own):
+            gt = ring.tile([P, 512, 4], BF16, name="grp", tag="grp", bufs=GRP, align_bytes=64)
+            src = raws[tile_key][:, :, 512 * h : 512 * h + 512].rearrange("p t (c i) -> p c t i", i=4)
+            dst = gt[:].rearrange("p (c i) t -> p c t i", i=4)
+            if own in "PQ":
+                for q in range(2):
+                    bk = pas.pop((key, q))
+                    part = gt[:, 256 * q : 256 * q + 256, :]
+                    if own == "P":
+                        nc.scalar.copy(out=part, in_=bk[:])
+                    else:
+                        nc.vector.tensor_copy(out=part, in_=bk[:])
+            elif own == "S":
+                nc.scalar.copy(out=dst, in_=src)
+            else:
+                nc.vector.tensor_copy(out=dst, in_=src)
+            groups[key] = gt
+
+        xc = one.tile([P, G, D], U32, name="xc", align_bytes=64)
+        xs = one.tile([P, G, D], U8, name="xs", align_bytes=64)
+
+        def x_il(u):
+            g, h = divmod(u, 2)
+            interleave(("x", u), ("x", g), h, X_OWN[u])
+            if h == 1:
+                next_load()
+
+        def x_q(u):
+            g, h = divmod(u, 2)
+            cols = slice(512 * h, 512 * h + 512)
+            nc.vector.quantize_mx(out=xc[:, g, cols].bitcast(E4), scales=xs[:, g, cols],
+                                  in_=groups[("x", u)][:].rearrange("p c t -> p (c t)"))
+
+        run = []
+
+        def half_max(g):
+            t = ring.tile([P, 2, S], BF16, name="mx1", tag="pre", bufs=3)
+            nc.vector.tensor_max(t[:], lg[g][:, 0:2, :], lg[g][:, 2:4, :])
+            return t
+
+        def pair_max(a, b, shape):
+            t = ring.tile(shape, BF16, name="mx2", tag="sil", bufs=3)
+            nc.vector.tensor_max(t[:], a, b)
+            return t
+
+        def all_max():
+            q0 = half_max(0)
+            q1 = half_max(1)
+            q2 = half_max(2)
+            q01 = pair_max(q0[:], q1[:], [P, 2, S])
+            q3 = half_max(3)
+            q012 = pair_max(q01[:], q2[:], [P, 2, S])
+            q = pair_max(q012[:], q3[:], [P, 2, S])
+            run.append(pair_max(q[:, 0, :], q[:, 1, :], [P, S]))
+
+        nmax = one.tile([P, E], F32, name="nmax")
+
+        def finish_max():
+            pt = bank([P, E, P], BF16)
+            for b in range(E):
+                nc.tensor.transpose(pt[:, b, :], run[-1][:, P * b : P * b + P], ident[:])
+            mx = one.tile([P, E], F32, name="mx")
+            nc.vector.tensor_reduce(out=mx[:], in_=pt[:], axis=AX.X, op=ALU.max)
+            nc.vector.tensor_scalar_mul(nmax[:], mx[:], -1.0)
+
+        lts, ats, bts, bgs = {}, {}, {}, {}
+        tot = one.tile([P, E, G], F32, name="tot")
+        bc = one.tile([P, E, G * P], U32, name="bc", align_bytes=64)
+        bs = one.tile([P, E, G * P], U8, name="bs", align_bytes=64)
+
+        def lt(s):
+            b, g = divmod(s, G)
+            lts[s] = bank([P, 4, P], BF16)
+            for j in range(4):
+                nc.tensor.transpose(lts[s][:, j, :], lg[g][:, j, P * b : P * b + P], ident[:])
+
+        def ex(s):
+            b, g = divmod(s, G)
+            at = ring.tile([P, 4, P], F32, name="at", tag="at", bufs=4)
+            nc.scalar.activation(at[:], lts[s][:], ACT.Exp, bias=nmax[:, b : b + 1], accum_out=tot[:, b, g : g + 1])
+            ats[s] = at
+
+        def bt(s):
+            bts[s] = bank([P, 4, P], F32)
+            for j in range(4):
+                nc.tensor.transpose(bts[s][:, j, :], ats[s][:, j, :], ident32[:])
+
+        def mult(s):
+            b, g = divmod(s, G)
+            if g == 0:
+                bgs[b] = ring.tile([P, G, P, 4], BF16, name="bgr", tag="bgr", bufs=2, align_bytes=64)
+            nc.vector.tensor_mul(bgs[b][:, g], bts[s][:].rearrange("p j n -> p n j"),
+                                 gain[:, g, :].unsqueeze(1).to_broadcast([P, P, 4]))
+
+        tsum = one.tile([P, E], F32, name="tsum")
+        rt = one.tile([P, E], F32, name="rt")
+
+        def bq(b):
+            nc.vector.quantize_mx(out=bc[:, b, :].bitcast(E4), scales=bs[:, b, :],
+                                  in_=bgs[b][:].rearrange("p g n j -> p (g n j)"))
+
+        mixes, slot, zs, zgs = {}, {}, {}, {}
+        ss = one.tile([P, E], F32, name="ss")
+        rstd = one.tile([P, E], F32, name="rstd")
+        zc = one.tile([P, E, 2 * P], U32, name="zc", align_bytes=64)
+        zsc = one.tile([P, E, 2 * P], U8, name="zsc", align_bytes=64)
+
+        def stage1(b):
+            for h in range(2):
+                acc = bank([P, 512], F32)
+                cols = slice(512 * h, 512 * h + 512)
+                for g in range(G):
+                    rows = slice(P * g, P * g + P)
+                    nc.tensor.matmul_mx(out=acc[:], lhsT=bc[:, b, rows].bitcast(E4), lhsT_scale=bs[:, b, rows],
+                                        rhs=xc[:, g, cols].bitcast(E4), rhs_scale=xs[:, g, cols],
+                                        start=(g == 0), stop=(g == G - 1))
+                mixes[(b, h)] = acc
+
+        def slots(b):
+            slot[b] = ring.tile([P, D], F32, name="slot", tag="slot", bufs=2)
+            for h in range(2):
+                cols = slice(512 * h, 512 * h + 512)
+                nc.vector.scalar_tensor_tensor(out=slot[b][:, cols], in0=mixes[(b, h)][:], scalar=rt[:, b : b + 1],
+                                               in1=emb[:, b, cols], op0=ALU.mult, op1=ALU.add)
+
+        def norm(b):
+            junk = ring.tile([P, D], BF16, name="junk", tag="junk", bufs=1)
+            nc.scalar.activation(junk[:], slot[b][:], ACT.Square, scale=1.0 / 32.0, accum_out=ss[:, b : b + 1])
+            nc.gpsimd.tensor_tensor(out=rstd[:, b : b + 1], in0=ss[:, b : b + 1], in1=mhalf[:], op=ALU.pow)
+
+        def zmake(b):
+            zs[b] = z = ring.tile([P, D], BF16, name="z", tag="z", bufs=2)
+            nc.vector.scalar_tensor_tensor(out=z[:], in0=slot[b][:], scalar=rstd[:, b : b + 1],
+                                           in1=ng[:, D * b : D * b + D], op0=ALU.mult, op1=ALU.mult)
+
+        def zturn(b):
+            words = zs[b][:].bitcast(F32)
+            zt = bank([P, 2, 2, P], F32)
+            for c in range(2):
+                for u in range(2):
+                    nc.tensor.transpose(zt[:, c, u, :], words[:, 256 * c + u : 256 * (c + 1) : 2], ident32[:])
+            zs[b] = zt
+
+        def zcopy(b):
+            zg = ring.tile([P, 2, P, 4], BF16, name="zg", tag="zg", bufs=2, align_bytes=64)
+            nc.scalar.copy(out=zg[:].rearrange("p c n t -> p (c n t)").bitcast(F32).rearrange("p (c n u) -> p c n u", c=2, u=2),
+                           in_=zs[b][:].rearrange("p c u n -> p c n u"))
+            zgs[b] = zg
+
+        def zq(b):
+            nc.vector.quantize_mx(out=zc[:, b, :].bitcast(E5), scales=zsc[:, b, :],
+                                  in_=zgs[b][:].rearrange("p c n t -> p (c n t)"))
+
+        codes, accs, pres, sils = {}, {}, {}, {}
+
+        def w_il(i):
+            interleave(("w", i), ("w", i // 2), i % 2, W_OWN[i])
+            if i % 2 == 1:
+                next_load()
+
+        def w_q(i):
+            c = ring.tile([P, 512], U32, name="wc", tag="wc", bufs=10, align_bytes=64)
+            s = ring.tile([P, 512], U8, name="ws", tag="ws", bufs=10, align_bytes=64)
+            nc.vector.quantize_mx(out=c[:].bitcast(E4), scales=s[:], in_=groups[("w", i)][:].rearrange("p c t -> p (c t)"))
+            codes[i] = (c, s)
+
+        def mm(i):
+            e, r = divmod(i, 8)
+            m, r = divmod(r, 4)
+            c, h = divmod(r, 2)
+            if c == 0:
+                accs[(e, m, h)] = bank([P, 512], F32)
+            zcols = slice(P * c, P * c + P)
+            nc.tensor.matmul_mx(out=accs[(e, m, h)][:], lhsT=zc[:, e, zcols].bitcast(E5), lhsT_scale=zsc[:, e, zcols],
+                                rhs=codes[i][0][:].bitcast(E4), rhs_scale=codes[i][1][:], start=(c == 0), stop=(c == 1))
+
+        def badd(e, h):
+            pres[(e, h)] = t = ring.tile([P, 512], F32, name="pre", tag="pre", bufs=3)
+            nc.vector.tensor_add(t[:], accs[(e, 0, h)][:], bg[:, F * e + 512 * h : F * e + 512 * h + 512])
+
+        def silu(e, h):
+            sl = ring.tile([P, 512], F32, name="sil", tag="sil", bufs=3)
+            nc.scalar.activation(sl[:], pres[(e, h)][:], ACT.Silu)
+            sils[(e, h)] = sl
+
+        def prod(e, h):
+            o = ring.tile([P, 512], F32, name="o", tag="o", bufs=3)
+            nc.vector.tensor_mul(o[:], accs[(e, 1, h)][:], sils[(e, h)][:])
+            nc.sync.dma_start(out=out[e, :, 512 * h : 512 * h + 512], in_=o[:])
+
+        ctx.enter_context(tc.manual_schedule())
+        lt(0)
+        lt(1)
+        for u in range(8):
+            if X_IL[u] == -2:
+                x_il(u)
+        all_max()
+        finish_max()
+        for s in range(-1, 16):
+            if 0 <= s + 2 < 16 and s + 2 > 1:
+                lt(s + 2)
+            if s >= 0:
+                ex(s)
+            for u in range(8):
+                if X_IL[u] == s:
+                    x_il(u)
+            if s >= 0:
+                bt(s)
+            if s >= 1:
+                mult(s - 1)
+            for u in range(8):
+                if X_Q[u] == s:
+                    x_q(u)
+            if s in (5, 9, 13):
+                bq(s // 4 - 1)
+        w_il(0)
+        mult(15)
+        for u in range(8):
+            if X_Q[u] >= 16:
+                x_q(u)
+        nc.vector.tensor_reduce(out=tsum[:], in_=tot[:], axis=AX.X, op=ALU.add)
+        bq(3)
+        nc.vector.reciprocal(rt[:], tsum[:])
+        w_il(1)
+        for b in range(E):
+            stage1(b)
+
+        due = {}
+
+        def at(step, fn, *args):
+            due.setdefault(step, []).append((fn, args))
+
+        for b in range(E):
+            k = 2 + D_SLOT[b]
+            at(k, slots, b)
+            at(k, norm, b)
+            at(k + 2, zmake, b)
+            at(k + 2, zturn, b)
+            at(k + 3, zcopy, b)
+            at(k + 4, zq, b)
+        z_step = [2 + D_SLOT[b] + 4 for b in range(E)]
+
+        def mm_at(n, step):
+            e, r = divmod(n, 8)
+            mm(n)
+            if r in (2, 3):
+                at(step + 1, badd, e, r - 2)
+                at(step + 2, silu, e, r - 2)
+            if r in (6, 7):
+                at(step + (1 if n < 30 else 0), prod, e, r - 6)
+
+        pend = []
+        i = 2
+        while i < 32 + LAG or due or pend:
+            if i + 1 < 32 and W_OWN[i + 1] in "PQ":
+                pass_through(("w", i + 1), ("w", (i + 1) // 2), (i + 1) % 2)
+            if i < 32:
+                w_il(i)
+            k = i - LAG
+            if 0 <= k < 32:
+                w_q(k)
+                pend.append(k)
+            for fn, args in due.pop(i, []):
+                fn(*args)
+            while pend and i >= z_step[pend[0] // 8]:
+                mm_at(pend.pop(0), i)
+            for fn, args in due.pop(i, []):
+                fn(*args)
+            i += 1

@@ -18,13 +18,15 @@ S = E * P
 G = T // 512
 FLOPS = 2 * T * S * D + 4 * S * D * F
 
-X_OWN = 'SSVVSVSV'
-W_OWN = 'SSSSSVVSVVVSSSVSVSVSSVSSVVSVSSVS'
-X_IL = [-2,-2,0,0,4,9,12,15]
-X_Q = [5,3,3,2,16,10,12,16]
+OWN = 'SSSVVSVSVSSSVSVSSSVVSSVSVSVSSVVSVVSSSSVS'
+EXP = [3,3,4,4,5,8,8,8]
+S1 = [10,13,13,16]
+SL = [13,16,16,18]
 LAG = 2
-GRP = 7
-D_SLOT = [0,1,3,4]
+OFF = [2,3,5,1,2,4]
+MAXT = 1
+LTL = 3
+GRP = 9
 
 
 def tile_soft_moe_dispatch_f3_kernel(tc, logits, token_gain, x, slot_embed, norm_gain, w_gate, b_gate, w_up, out):
@@ -55,7 +57,7 @@ def tile_soft_moe_dispatch_f3_kernel(tc, logits, token_gain, x, slot_embed, norm
         raws = {}
 
         def load_raw(key, src, split=False):
-            r = ring.tile([P, 4, 1024], BF16, name="raw", tag="raw", bufs=6)
+            r = ring.tile([P, 4, 1024], BF16, name="raw", tag="raw", bufs=5)
             if split:
                 nc.sync.dma_start(out=r[:, :, 0:512], in_=src[:, :, 0:512])
             else:
@@ -92,33 +94,15 @@ def tile_soft_moe_dispatch_f3_kernel(tc, logits, token_gain, x, slot_embed, norm
                 loaded.append(i)
 
         next_load()
-        next_load()
         nc.sync.dma_start(out=bg[:], in_=b_gate.rearrange("e d -> (e d)").partition_broadcast(P))
 
         groups = {}
-        pas = {}
-
-        def pass_through(key, tile_key, h):
-            for q in range(2):
-                bk = bank([P, 256, 4], BF16)
-                c0 = 512 * h + 256 * q
-                for j in range(4):
-                    nc.tensor.matmul(bk[:, :, j], lhsT=ident[:], rhs=raws[tile_key][:, j, c0 : c0 + 256], start=True, stop=True)
-                pas[(key, q)] = bk
 
         def interleave(key, tile_key, h, own):
             gt = ring.tile([P, 512, 4], BF16, name="grp", tag="grp", bufs=GRP, align_bytes=64)
             src = raws[tile_key][:, :, 512 * h : 512 * h + 512].rearrange("p t (c i) -> p c t i", i=4)
             dst = gt[:].rearrange("p (c i) t -> p c t i", i=4)
-            if own in "PQ":
-                for q in range(2):
-                    bk = pas.pop((key, q))
-                    part = gt[:, 256 * q : 256 * q + 256, :]
-                    if own == "P":
-                        nc.scalar.copy(out=part, in_=bk[:])
-                    else:
-                        nc.vector.tensor_copy(out=part, in_=bk[:])
-            elif own == "S":
+            if own == "S":
                 nc.scalar.copy(out=dst, in_=src)
             else:
                 nc.vector.tensor_copy(out=dst, in_=src)
@@ -129,7 +113,7 @@ def tile_soft_moe_dispatch_f3_kernel(tc, logits, token_gain, x, slot_embed, norm
 
         def x_il(u):
             g, h = divmod(u, 2)
-            interleave(("x", u), ("x", g), h, X_OWN[u])
+            interleave(("x", u), ("x", g), h, OWN[u])
             if h == 1:
                 next_load()
 
@@ -172,33 +156,37 @@ def tile_soft_moe_dispatch_f3_kernel(tc, logits, token_gain, x, slot_embed, norm
             nc.vector.tensor_scalar_mul(nmax[:], mx[:], -1.0)
 
         lts, ats, bts, bgs = {}, {}, {}, {}
-        tot = one.tile([P, E, G], F32, name="tot")
+        tot = one.tile([P, E, 2], F32, name="tot")
         bc = one.tile([P, E, G * P], U32, name="bc", align_bytes=64)
         bs = one.tile([P, E, G * P], U8, name="bs", align_bytes=64)
 
-        def lt(s):
-            b, g = divmod(s, G)
-            lts[s] = bank([P, 4, P], BF16)
-            for j in range(4):
-                nc.tensor.transpose(lts[s][:, j, :], lg[g][:, j, P * b : P * b + P], ident[:])
+        def lt(k):
+            b, q = divmod(k, 2)
+            lts[k] = bank([P, 2, 4, P], BF16)
+            for r in range(2):
+                for j in range(4):
+                    nc.tensor.transpose(lts[k][:, r, j, :], lg[2 * q + r][:, j, P * b : P * b + P], ident[:])
 
-        def ex(s):
-            b, g = divmod(s, G)
-            at = ring.tile([P, 4, P], F32, name="at", tag="at", bufs=4)
-            nc.scalar.activation(at[:], lts[s][:], ACT.Exp, bias=nmax[:, b : b + 1], accum_out=tot[:, b, g : g + 1])
-            ats[s] = at
+        def ex(k):
+            b, q = divmod(k, 2)
+            at = ring.tile([P, 2, 4, P], F32, name="at", tag="at", bufs=2)
+            nc.scalar.activation(at[:], lts[k][:], ACT.Exp, bias=nmax[:, b : b + 1], accum_out=tot[:, b, q : q + 1])
+            ats[k] = at
 
-        def bt(s):
-            bts[s] = bank([P, 4, P], F32)
-            for j in range(4):
-                nc.tensor.transpose(bts[s][:, j, :], ats[s][:, j, :], ident32[:])
+        def bt(k):
+            for r in range(2):
+                bts[(k, r)] = bank([P, 4, P], F32)
+                for j in range(4):
+                    nc.tensor.transpose(bts[(k, r)][:, j, :], ats[k][:, r, j, :], ident32[:])
 
-        def mult(s):
-            b, g = divmod(s, G)
-            if g == 0:
+        def mult(k):
+            b, q = divmod(k, 2)
+            if q == 0:
                 bgs[b] = ring.tile([P, G, P, 4], BF16, name="bgr", tag="bgr", bufs=2, align_bytes=64)
-            nc.vector.tensor_mul(bgs[b][:, g], bts[s][:].rearrange("p j n -> p n j"),
-                                 gain[:, g, :].unsqueeze(1).to_broadcast([P, P, 4]))
+            for r in range(2):
+                g = 2 * q + r
+                nc.vector.tensor_mul(bgs[b][:, g], bts[(k, r)][:].rearrange("p j n -> p n j"),
+                                     gain[:, g, :].unsqueeze(1).to_broadcast([P, P, 4]))
 
         tsum = one.tile([P, E], F32, name="tsum")
         rt = one.tile([P, E], F32, name="rt")
@@ -262,7 +250,7 @@ def tile_soft_moe_dispatch_f3_kernel(tc, logits, token_gain, x, slot_embed, norm
         codes, accs, pres, sils = {}, {}, {}, {}
 
         def w_il(i):
-            interleave(("w", i), ("w", i // 2), i % 2, W_OWN[i])
+            interleave(("w", i), ("w", i // 2), i % 2, OWN[8 + i])
             if i % 2 == 1:
                 next_load()
 
@@ -297,81 +285,67 @@ def tile_soft_moe_dispatch_f3_kernel(tc, logits, token_gain, x, slot_embed, norm
             nc.sync.dma_start(out=out[e, :, 512 * h : 512 * h + 512], in_=o[:])
 
         ctx.enter_context(tc.manual_schedule())
-        lt(0)
-        lt(1)
-        for u in range(8):
-            if X_IL[u] == -2:
-                x_il(u)
-        all_max()
-        finish_max()
-        for s in range(-1, 16):
-            if 0 <= s + 2 < 16 and s + 2 > 1:
-                lt(s + 2)
-            if s >= 0:
-                ex(s)
-            for u in range(8):
-                if X_IL[u] == s:
-                    x_il(u)
-            if s >= 0:
-                bt(s)
-            if s >= 1:
-                mult(s - 1)
-            for u in range(8):
-                if X_Q[u] == s:
-                    x_q(u)
-            if s in (5, 9, 13):
-                bq(s // 4 - 1)
-        w_il(0)
-        mult(15)
-        for u in range(8):
-            if X_Q[u] >= 16:
-                x_q(u)
-        nc.vector.tensor_reduce(out=tsum[:], in_=tot[:], axis=AX.X, op=ALU.add)
-        bq(3)
-        nc.vector.reciprocal(rt[:], tsum[:])
-        w_il(1)
-        for b in range(E):
-            stage1(b)
-
         due = {}
 
         def at(step, fn, *args):
             due.setdefault(step, []).append((fn, args))
 
+        def totals():
+            nc.vector.tensor_reduce(out=tsum[:], in_=tot[:], axis=AX.X, op=ALU.add)
+
+        def inverse():
+            nc.vector.reciprocal(rt[:], tsum[:])
+
+        at(MAXT, all_max)
+        at(MAXT, finish_max)
+        for k in range(8):
+            at(max(0, EXP[k] - LTL), lt, k)
+        for k in range(8):
+            at(EXP[k], ex, k)
+            at(EXP[k], bt, k)
+            at(EXP[k] + 1, mult, k)
+            if k % 2:
+                at(EXP[k] + 2, bq, k // 2)
+        at(EXP[7] + 1, totals)
+        at(EXP[7] + 2, inverse)
+        z_step = []
         for b in range(E):
-            k = 2 + D_SLOT[b]
-            at(k, slots, b)
-            at(k, norm, b)
-            at(k + 2, zmake, b)
-            at(k + 2, zturn, b)
-            at(k + 3, zcopy, b)
-            at(k + 4, zq, b)
-        z_step = [2 + D_SLOT[b] + 4 for b in range(E)]
+            at(S1[b], stage1, b)
+            at(SL[b], slots, b)
+            at(SL[b], norm, b)
+            at(SL[b] + OFF[0], zmake, b)
+            at(SL[b] + OFF[0], zturn, b)
+            at(SL[b] + OFF[1], zcopy, b)
+            at(SL[b] + OFF[2], zq, b)
+            z_step.append(SL[b] + OFF[2])
 
         def mm_at(n, step):
             e, r = divmod(n, 8)
             mm(n)
             if r in (2, 3):
-                at(step + 1, badd, e, r - 2)
-                at(step + 2, silu, e, r - 2)
+                at(step + OFF[3], badd, e, r - 2)
+                at(step + OFF[4], silu, e, r - 2)
             if r in (6, 7):
-                at(step + (1 if n < 30 else 0), prod, e, r - 6)
+                at(step + (OFF[5] if n < 30 else 0), prod, e, r - 6)
 
         pend = []
-        i = 2
-        while i < 32 + LAG or due or pend:
-            if i + 1 < 32 and W_OWN[i + 1] in "PQ":
-                pass_through(("w", i + 1), ("w", (i + 1) // 2), (i + 1) % 2)
-            if i < 32:
-                w_il(i)
-            k = i - LAG
-            if 0 <= k < 32:
-                w_q(k)
-                pend.append(k)
-            for fn, args in due.pop(i, []):
+        step = 0
+        while step < 40 + LAG or due or pend:
+            if step < 8:
+                x_il(step)
+            elif step < 40:
+                w_il(step - 8)
+            events = due.pop(step, [])
+            for fn, args in events:
                 fn(*args)
-            while pend and i >= z_step[pend[0] // 8]:
-                mm_at(pend.pop(0), i)
-            for fn, args in due.pop(i, []):
+            k = step - LAG
+            if 0 <= k < 8:
+                x_q(k)
+            elif 8 <= k < 40:
+                w_q(k - 8)
+                pend.append(k - 8)
+            while pend and step >= z_step[pend[0] // 8]:
+                mm_at(pend.pop(0), step)
+            for fn, args in due.pop(step, []):
                 fn(*args)
-            i += 1
+            step += 1

@@ -18,11 +18,13 @@ S = E * P
 G = T // 512
 FLOPS = 2 * T * S * D + 4 * S * D * F
 
-OWN = 'SSSVVSVSVSSSVSVSSSVVSSVSVSVSSVVSVVSSSSVS'
-EXP = [3,3,4,4,5,8,8,8]
-S1 = [10,13,13,16]
+OWN = 'SSVSVVSSVVSSSSSVSSVVSSVSVPPVSSVSVPPVSSVS'
+EXP = [3,3,5,5,7,7,8,9]
+S1 = [10,10,11,16]
 SL = [13,16,16,18]
 LAG = 2
+PLEAD = 3
+HEAD = 'aggggbdc'
 OFF = [2,3,5,1,2,4]
 MAXT = 1
 LTL = 3
@@ -44,7 +46,6 @@ def tile_soft_moe_dispatch_f3_kernel(tc, logits, token_gain, x, slot_embed, norm
         warm2 = one.tile([P, 1], F32, name="warm2")
         nc.scalar.activation(warm2[:], warm[:], ACT.Exp)
         gain = one.tile([P, G, 4], BF16, name="gain")
-        nc.scalar.dma_start(out=gain[:], in_=token_gain.rearrange("(g p j) -> p g j", p=P, j=4))
         ident = one.tile([P, P], BF16, name="ident")
         make_identity(nc, ident[:])
         ident32 = one.tile([P, P], F32, name="ident32")
@@ -56,22 +57,25 @@ def tile_soft_moe_dispatch_f3_kernel(tc, logits, token_gain, x, slot_embed, norm
         lv = logits.rearrange("(g p j) s -> g p j s", p=P, j=4)
         raws = {}
 
-        def load_raw(key, src, split=False):
+        def load_raw(key, src):
             r = ring.tile([P, 4, 1024], BF16, name="raw", tag="raw", bufs=5)
-            if split:
-                nc.sync.dma_start(out=r[:, :, 0:512], in_=src[:, :, 0:512])
-            else:
-                nc.sync.dma_start(out=r[:], in_=src)
-            raws[key] = r
+            nc.sync.dma_start(out=r[:], in_=src)
+            raws[(key, 0)] = r[:, :, 0:512]
+            raws[(key, 1)] = r[:, :, 512:1024]
 
         lg = []
-        load_raw(("x", 0), xv[0], split=True)
-        for g in range(G):
-            t = one.tile([P, 4, S], BF16, name="lg%d" % g)
-            nc.sync.dma_start(out=t[:], in_=lv[g])
-            lg.append(t)
-        nc.sync.dma_start(out=raws[("x", 0)][:, :, 512:1024], in_=xv[0][:, :, 512:1024])
-        for g in range(1, G):
+        for c in HEAD:
+            if c == "g":
+                t = one.tile([P, 4, S], BF16, name="lg%d" % len(lg))
+                nc.sync.dma_start(out=t[:], in_=lv[len(lg)])
+                lg.append(t)
+            else:
+                g, h = divmod("abcd".index(c), 2)
+                r = ring.tile([P, 4, 512], BF16, name="grp", tag="grp", bufs=GRP, align_bytes=64)
+                nc.sync.dma_start(out=r[:], in_=xv[g][:, :, 512 * h : 512 * h + 512])
+                raws[(("x", g), h)] = r
+        nc.sync.dma_start(out=gain[:], in_=token_gain.rearrange("(g p j) -> p g j", p=P, j=4))
+        for g in range(2, G):
             load_raw(("x", g), xv[g])
         emb = one.tile([P, E, D], BF16, name="emb")
         nc.sync.dma_start(out=emb[:], in_=slot_embed.rearrange("(e p) d -> p e d", p=P))
@@ -94,15 +98,34 @@ def tile_soft_moe_dispatch_f3_kernel(tc, logits, token_gain, x, slot_embed, norm
                 loaded.append(i)
 
         next_load()
+        next_load()
+        next_load()
         nc.sync.dma_start(out=bg[:], in_=b_gate.rearrange("e d -> (e d)").partition_broadcast(P))
 
         groups = {}
+        pas = {}
+
+        def pass_through(key, tile_key, h):
+            for q in range(2):
+                bk = bank([P, 256, 4], BF16)
+                for r in range(2):
+                    c0 = 256 * q + 128 * r
+                    nc.tensor.matmul(bk[:, 128 * r : 128 * r + 128, :].rearrange("p c t -> p (c t)"), lhsT=ident[:],
+                                     rhs=raws[(tile_key, h)][:, :, c0 : c0 + 128].rearrange("p t c -> p c t"), start=True, stop=True)
+                pas[(key, q)] = bk
 
         def interleave(key, tile_key, h, own):
             gt = ring.tile([P, 512, 4], BF16, name="grp", tag="grp", bufs=GRP, align_bytes=64)
-            src = raws[tile_key][:, :, 512 * h : 512 * h + 512].rearrange("p t (c i) -> p c t i", i=4)
+            src = raws[(tile_key, h)][:, :, :].rearrange("p t (c i) -> p c t i", i=4)
             dst = gt[:].rearrange("p (c i) t -> p c t i", i=4)
-            if own == "S":
+            if own in "PQ":
+                for q in range(2):
+                    part = gt[:, 256 * q : 256 * q + 256, :]
+                    if own == "P":
+                        nc.scalar.copy(out=part, in_=pas[(key, q)][:])
+                    else:
+                        nc.vector.tensor_copy(out=part, in_=pas[(key, q)][:])
+            elif own == "S":
                 nc.scalar.copy(out=dst, in_=src)
             else:
                 nc.vector.tensor_copy(out=dst, in_=src)
@@ -114,7 +137,7 @@ def tile_soft_moe_dispatch_f3_kernel(tc, logits, token_gain, x, slot_embed, norm
         def x_il(u):
             g, h = divmod(u, 2)
             interleave(("x", u), ("x", g), h, OWN[u])
-            if h == 1:
+            if h == 1 and g >= 2:
                 next_load()
 
         def x_q(u):
@@ -280,9 +303,11 @@ def tile_soft_moe_dispatch_f3_kernel(tc, logits, token_gain, x, slot_embed, norm
             sils[(e, h)] = sl
 
         def prod(e, h):
-            o = ring.tile([P, 512], F32, name="o", tag="o", bufs=3)
-            nc.vector.tensor_mul(o[:], accs[(e, 1, h)][:], sils[(e, h)][:])
-            nc.sync.dma_start(out=out[e, :, 512 * h : 512 * h + 512], in_=o[:])
+            width = 256 if (e, h) == (E - 1, 1) else 512
+            for c in range(0, 512, width):
+                o = ring.tile([P, width], F32, name="o", tag="o", bufs=3)
+                nc.vector.tensor_mul(o[:], accs[(e, 1, h)][:, c : c + width], sils[(e, h)][:, c : c + width])
+                nc.sync.dma_start(out=out[e, :, 512 * h + c : 512 * h + c + width], in_=o[:])
 
         ctx.enter_context(tc.manual_schedule())
         due = {}
@@ -331,6 +356,9 @@ def tile_soft_moe_dispatch_f3_kernel(tc, logits, token_gain, x, slot_embed, norm
         pend = []
         step = 0
         while step < 40 + LAG or due or pend:
+            if 8 <= step + PLEAD < 40 and OWN[step + PLEAD] in "PQ":
+                i = step + PLEAD - 8
+                pass_through(("w", i), ("w", i // 2), i % 2)
             if step < 8:
                 x_il(step)
             elif step < 40:

from contextlib import ExitStack

import concourse.mybir as mybir
from concourse.masks import make_identity

F32 = mybir.dt.float32
BF16 = mybir.dt.bfloat16
U32 = mybir.dt.uint32
U8 = mybir.dt.uint8
E4 = mybir.dt.float8_e4m3fn_x4
E5 = mybir.dt.float8_e5m2_x4
ACT = mybir.ActivationFunctionType
ALU = mybir.AluOpType
AX = mybir.AxisListType

T, E, P, D, F = 2048, 4, 128, 1024, 1024
S = E * P
G = T // 512
FLOPS = 2 * T * S * D + 4 * S * D * F

OWN = 'SSVSVVSSVVSSSSSVSSVVSSVSVPPVSSVSVPPVSSVS'
EXP = [3,3,5,5,7,7,8,9]
S1 = [10,10,11,16]
SL = [13,16,16,18]
LAG = 2
PLEAD = 3
HEAD = 'aggggbdc'
OFF = [2,3,5,1,2,4]
MAXT = 1
LTL = 3
GRP = 9


def tile_soft_moe_dispatch_f3_kernel(tc, logits, token_gain, x, slot_embed, norm_gain, w_gate, b_gate, w_up, out):
    nc = tc.nc
    with ExitStack() as ctx:
        one = ctx.enter_context(tc.tile_pool(name="one", bufs=1))
        ring = ctx.enter_context(tc.tile_pool(name="ring", bufs=2))
        psum = ctx.enter_context(tc.psum_pool(name="psum", bufs=8))

        def bank(shape, dtype):
            return psum.tile(shape, dtype, name="bank", tag="bank", bufs=8)

        warm = one.tile([P, 1], F32, name="warm")
        nc.vector.memset(warm[:], 0.0)
        warm2 = one.tile([P, 1], F32, name="warm2")
        nc.scalar.activation(warm2[:], warm[:], ACT.Exp)
        gain = one.tile([P, G, 4], BF16, name="gain")
        ident = one.tile([P, P], BF16, name="ident")
        make_identity(nc, ident[:])
        ident32 = one.tile([P, P], F32, name="ident32")
        make_identity(nc, ident32[:])
        mhalf = one.tile([P, 1], F32, name="mhalf")
        nc.gpsimd.memset(mhalf[:], -0.5)

        xv = x.rearrange("(g p j) d -> g p j d", p=P, j=4)
        lv = logits.rearrange("(g p j) s -> g p j s", p=P, j=4)
        raws = {}

        def load_raw(key, src):
            r = ring.tile([P, 4, 1024], BF16, name="raw", tag="raw", bufs=5)
            nc.sync.dma_start(out=r[:], in_=src)
            raws[(key, 0)] = r[:, :, 0:512]
            raws[(key, 1)] = r[:, :, 512:1024]

        lg = []
        for c in HEAD:
            if c == "g":
                t = one.tile([P, 4, S], BF16, name="lg%d" % len(lg))
                nc.sync.dma_start(out=t[:], in_=lv[len(lg)])
                lg.append(t)
            else:
                g, h = divmod("abcd".index(c), 2)
                r = ring.tile([P, 4, 512], BF16, name="grp", tag="grp", bufs=GRP, align_bytes=64)
                nc.sync.dma_start(out=r[:], in_=xv[g][:, :, 512 * h : 512 * h + 512])
                raws[(("x", g), h)] = r
        nc.sync.dma_start(out=gain[:], in_=token_gain.rearrange("(g p j) -> p g j", p=P, j=4))
        for g in range(2, G):
            load_raw(("x", g), xv[g])
        emb = one.tile([P, E, D], BF16, name="emb")
        nc.sync.dma_start(out=emb[:], in_=slot_embed.rearrange("(e p) d -> p e d", p=P))
        ng = one.tile([P, E * D], BF16, name="ng")
        nc.sync.dma_start(out=ng[:], in_=norm_gain.rearrange("e d -> (e d)").partition_broadcast(P))
        bg = one.tile([P, E * F], BF16, name="bg")

        wsrc = []
        for e in range(E):
            for m, w in enumerate((w_gate, w_up)):
                wv = w[e].rearrange("(c p j) f -> c p j f", p=P, j=4)
                for c in range(2):
                    wsrc.append(wv[c])
        loaded = []

        def next_load():
            i = len(loaded)
            if i < len(wsrc):
                load_raw(("w", i), wsrc[i])
                loaded.append(i)

        next_load()
        next_load()
        next_load()
        nc.sync.dma_start(out=bg[:], in_=b_gate.rearrange("e d -> (e d)").partition_broadcast(P))

        groups = {}
        pas = {}

        def pass_through(key, tile_key, h):
            for q in range(2):
                bk = bank([P, 256, 4], BF16)
                for r in range(2):
                    c0 = 256 * q + 128 * r
                    nc.tensor.matmul(bk[:, 128 * r : 128 * r + 128, :].rearrange("p c t -> p (c t)"), lhsT=ident[:],
                                     rhs=raws[(tile_key, h)][:, :, c0 : c0 + 128].rearrange("p t c -> p c t"), start=True, stop=True)
                pas[(key, q)] = bk

        def interleave(key, tile_key, h, own):
            gt = ring.tile([P, 512, 4], BF16, name="grp", tag="grp", bufs=GRP, align_bytes=64)
            src = raws[(tile_key, h)][:, :, :].rearrange("p t (c i) -> p c t i", i=4)
            dst = gt[:].rearrange("p (c i) t -> p c t i", i=4)
            if own in "PQ":
                for q in range(2):
                    part = gt[:, 256 * q : 256 * q + 256, :]
                    if own == "P":
                        nc.scalar.copy(out=part, in_=pas[(key, q)][:])
                    else:
                        nc.vector.tensor_copy(out=part, in_=pas[(key, q)][:])
            elif own == "S":
                nc.scalar.copy(out=dst, in_=src)
            else:
                nc.vector.tensor_copy(out=dst, in_=src)
            groups[key] = gt

        xc = one.tile([P, G, D], U32, name="xc", align_bytes=64)
        xs = one.tile([P, G, D], U8, name="xs", align_bytes=64)

        def x_il(u):
            g, h = divmod(u, 2)
            interleave(("x", u), ("x", g), h, OWN[u])
            if h == 1 and g >= 2:
                next_load()

        def x_q(u):
            g, h = divmod(u, 2)
            cols = slice(512 * h, 512 * h + 512)
            nc.vector.quantize_mx(out=xc[:, g, cols].bitcast(E4), scales=xs[:, g, cols],
                                  in_=groups[("x", u)][:].rearrange("p c t -> p (c t)"))

        run = []

        def half_max(g):
            t = ring.tile([P, 2, S], BF16, name="mx1", tag="pre", bufs=3)
            nc.vector.tensor_max(t[:], lg[g][:, 0:2, :], lg[g][:, 2:4, :])
            return t

        def pair_max(a, b, shape):
            t = ring.tile(shape, BF16, name="mx2", tag="sil", bufs=3)
            nc.vector.tensor_max(t[:], a, b)
            return t

        def all_max():
            q0 = half_max(0)
            q1 = half_max(1)
            q2 = half_max(2)
            q01 = pair_max(q0[:], q1[:], [P, 2, S])
            q3 = half_max(3)
            q012 = pair_max(q01[:], q2[:], [P, 2, S])
            q = pair_max(q012[:], q3[:], [P, 2, S])
            run.append(pair_max(q[:, 0, :], q[:, 1, :], [P, S]))

        nmax = one.tile([P, E], F32, name="nmax")

        def finish_max():
            pt = bank([P, E, P], BF16)
            for b in range(E):
                nc.tensor.transpose(pt[:, b, :], run[-1][:, P * b : P * b + P], ident[:])
            mx = one.tile([P, E], F32, name="mx")
            nc.vector.tensor_reduce(out=mx[:], in_=pt[:], axis=AX.X, op=ALU.max)
            nc.vector.tensor_scalar_mul(nmax[:], mx[:], -1.0)

        lts, ats, bts, bgs = {}, {}, {}, {}
        tot = one.tile([P, E, 2], F32, name="tot")
        bc = one.tile([P, E, G * P], U32, name="bc", align_bytes=64)
        bs = one.tile([P, E, G * P], U8, name="bs", align_bytes=64)

        def lt(k):
            b, q = divmod(k, 2)
            lts[k] = bank([P, 2, 4, P], BF16)
            for r in range(2):
                for j in range(4):
                    nc.tensor.transpose(lts[k][:, r, j, :], lg[2 * q + r][:, j, P * b : P * b + P], ident[:])

        def ex(k):
            b, q = divmod(k, 2)
            at = ring.tile([P, 2, 4, P], F32, name="at", tag="at", bufs=2)
            nc.scalar.activation(at[:], lts[k][:], ACT.Exp, bias=nmax[:, b : b + 1], accum_out=tot[:, b, q : q + 1])
            ats[k] = at

        def bt(k):
            for r in range(2):
                bts[(k, r)] = bank([P, 4, P], F32)
                for j in range(4):
                    nc.tensor.transpose(bts[(k, r)][:, j, :], ats[k][:, r, j, :], ident32[:])

        def mult(k):
            b, q = divmod(k, 2)
            if q == 0:
                bgs[b] = ring.tile([P, G, P, 4], BF16, name="bgr", tag="bgr", bufs=2, align_bytes=64)
            for r in range(2):
                g = 2 * q + r
                nc.vector.tensor_mul(bgs[b][:, g], bts[(k, r)][:].rearrange("p j n -> p n j"),
                                     gain[:, g, :].unsqueeze(1).to_broadcast([P, P, 4]))

        tsum = one.tile([P, E], F32, name="tsum")
        rt = one.tile([P, E], F32, name="rt")

        def bq(b):
            nc.vector.quantize_mx(out=bc[:, b, :].bitcast(E4), scales=bs[:, b, :],
                                  in_=bgs[b][:].rearrange("p g n j -> p (g n j)"))

        mixes, slot, zs, zgs = {}, {}, {}, {}
        ss = one.tile([P, E], F32, name="ss")
        rstd = one.tile([P, E], F32, name="rstd")
        zc = one.tile([P, E, 2 * P], U32, name="zc", align_bytes=64)
        zsc = one.tile([P, E, 2 * P], U8, name="zsc", align_bytes=64)

        def stage1(b):
            for h in range(2):
                acc = bank([P, 512], F32)
                cols = slice(512 * h, 512 * h + 512)
                for g in range(G):
                    rows = slice(P * g, P * g + P)
                    nc.tensor.matmul_mx(out=acc[:], lhsT=bc[:, b, rows].bitcast(E4), lhsT_scale=bs[:, b, rows],
                                        rhs=xc[:, g, cols].bitcast(E4), rhs_scale=xs[:, g, cols],
                                        start=(g == 0), stop=(g == G - 1))
                mixes[(b, h)] = acc

        def slots(b):
            slot[b] = ring.tile([P, D], F32, name="slot", tag="slot", bufs=2)
            for h in range(2):
                cols = slice(512 * h, 512 * h + 512)
                nc.vector.scalar_tensor_tensor(out=slot[b][:, cols], in0=mixes[(b, h)][:], scalar=rt[:, b : b + 1],
                                               in1=emb[:, b, cols], op0=ALU.mult, op1=ALU.add)

        def norm(b):
            junk = ring.tile([P, D], BF16, name="junk", tag="junk", bufs=1)
            nc.scalar.activation(junk[:], slot[b][:], ACT.Square, scale=1.0 / 32.0, accum_out=ss[:, b : b + 1])
            nc.gpsimd.tensor_tensor(out=rstd[:, b : b + 1], in0=ss[:, b : b + 1], in1=mhalf[:], op=ALU.pow)

        def zmake(b):
            zs[b] = z = ring.tile([P, D], BF16, name="z", tag="z", bufs=2)
            nc.vector.scalar_tensor_tensor(out=z[:], in0=slot[b][:], scalar=rstd[:, b : b + 1],
                                           in1=ng[:, D * b : D * b + D], op0=ALU.mult, op1=ALU.mult)

        def zturn(b):
            words = zs[b][:].bitcast(F32)
            zt = bank([P, 2, 2, P], F32)
            for c in range(2):
                for u in range(2):
                    nc.tensor.transpose(zt[:, c, u, :], words[:, 256 * c + u : 256 * (c + 1) : 2], ident32[:])
            zs[b] = zt

        def zcopy(b):
            zg = ring.tile([P, 2, P, 4], BF16, name="zg", tag="zg", bufs=2, align_bytes=64)
            nc.scalar.copy(out=zg[:].rearrange("p c n t -> p (c n t)").bitcast(F32).rearrange("p (c n u) -> p c n u", c=2, u=2),
                           in_=zs[b][:].rearrange("p c u n -> p c n u"))
            zgs[b] = zg

        def zq(b):
            nc.vector.quantize_mx(out=zc[:, b, :].bitcast(E5), scales=zsc[:, b, :],
                                  in_=zgs[b][:].rearrange("p c n t -> p (c n t)"))

        codes, accs, pres, sils = {}, {}, {}, {}

        def w_il(i):
            interleave(("w", i), ("w", i // 2), i % 2, OWN[8 + i])
            if i % 2 == 1:
                next_load()

        def w_q(i):
            c = ring.tile([P, 512], U32, name="wc", tag="wc", bufs=10, align_bytes=64)
            s = ring.tile([P, 512], U8, name="ws", tag="ws", bufs=10, align_bytes=64)
            nc.vector.quantize_mx(out=c[:].bitcast(E4), scales=s[:], in_=groups[("w", i)][:].rearrange("p c t -> p (c t)"))
            codes[i] = (c, s)

        def mm(i):
            e, r = divmod(i, 8)
            m, r = divmod(r, 4)
            c, h = divmod(r, 2)
            if c == 0:
                accs[(e, m, h)] = bank([P, 512], F32)
            zcols = slice(P * c, P * c + P)
            nc.tensor.matmul_mx(out=accs[(e, m, h)][:], lhsT=zc[:, e, zcols].bitcast(E5), lhsT_scale=zsc[:, e, zcols],
                                rhs=codes[i][0][:].bitcast(E4), rhs_scale=codes[i][1][:], start=(c == 0), stop=(c == 1))

        def badd(e, h):
            pres[(e, h)] = t = ring.tile([P, 512], F32, name="pre", tag="pre", bufs=3)
            nc.vector.tensor_add(t[:], accs[(e, 0, h)][:], bg[:, F * e + 512 * h : F * e + 512 * h + 512])

        def silu(e, h):
            sl = ring.tile([P, 512], F32, name="sil", tag="sil", bufs=3)
            nc.scalar.activation(sl[:], pres[(e, h)][:], ACT.Silu)
            sils[(e, h)] = sl

        def prod(e, h):
            width = 256 if (e, h) == (E - 1, 1) else 512
            for c in range(0, 512, width):
                o = ring.tile([P, width], F32, name="o", tag="o", bufs=3)
                nc.vector.tensor_mul(o[:], accs[(e, 1, h)][:, c : c + width], sils[(e, h)][:, c : c + width])
                nc.sync.dma_start(out=out[e, :, 512 * h + c : 512 * h + c + width], in_=o[:])

        ctx.enter_context(tc.manual_schedule())
        due = {}

        def at(step, fn, *args):
            due.setdefault(step, []).append((fn, args))

        def totals():
            nc.vector.tensor_reduce(out=tsum[:], in_=tot[:], axis=AX.X, op=ALU.add)

        def inverse():
            nc.vector.reciprocal(rt[:], tsum[:])

        at(MAXT, all_max)
        at(MAXT, finish_max)
        for k in range(8):
            at(max(0, EXP[k] - LTL), lt, k)
        for k in range(8):
            at(EXP[k], ex, k)
            at(EXP[k], bt, k)
            at(EXP[k] + 1, mult, k)
            if k % 2:
                at(EXP[k] + 2, bq, k // 2)
        at(EXP[7] + 1, totals)
        at(EXP[7] + 2, inverse)
        z_step = []
        for b in range(E):
            at(S1[b], stage1, b)
            at(SL[b], slots, b)
            at(SL[b], norm, b)
            at(SL[b] + OFF[0], zmake, b)
            at(SL[b] + OFF[0], zturn, b)
            at(SL[b] + OFF[1], zcopy, b)
            at(SL[b] + OFF[2], zq, b)
            z_step.append(SL[b] + OFF[2])

        def mm_at(n, step):
            e, r = divmod(n, 8)
            mm(n)
            if r in (2, 3):
                at(step + OFF[3], badd, e, r - 2)
                at(step + OFF[4], silu, e, r - 2)
            if r in (6, 7):
                at(step + (OFF[5] if n < 30 else 0), prod, e, r - 6)

        pend = []
        step = 0
        while step < 40 + LAG or due or pend:
            if 8 <= step + PLEAD < 40 and OWN[step + PLEAD] in "PQ":
                i = step + PLEAD - 8
                pass_through(("w", i), ("w", i // 2), i % 2)
            if step < 8:
                x_il(step)
            elif step < 40:
                w_il(step - 8)
            events = due.pop(step, [])
            for fn, args in events:
                fn(*args)
            k = step - LAG
            if 0 <= k < 8:
                x_q(k)
            elif 8 <= k < 40:
                w_q(k - 8)
                pend.append(k - 8)
            while pend and step >= z_step[pend[0] // 8]:
                mm_at(pend.pop(0), step)
            for fn, args in due.pop(step, []):
                fn(*args)
            step += 1
